import numpy as np
import ml_dtypes


def mxq(x, axis, fmt="e4m3"):
    dtype, down = {"e4m3": (ml_dtypes.float8_e4m3fn, 7), "e5m2": (ml_dtypes.float8_e5m2, 14)}[fmt]
    v = np.moveaxis(np.asarray(x, np.float32).astype(ml_dtypes.bfloat16).astype(np.float64), axis, -1)
    blocks = v.reshape(v.shape[:-1] + (-1, 32))
    amax = np.abs(blocks).max(-1, keepdims=True)
    byte = np.maximum(np.where(amax > 0, np.frexp(amax)[1] - 1 + 127, 0) - down, 1)
    scale = np.exp2(byte - 127.0)
    codes = (blocks / scale).astype(np.float32).astype(dtype).astype(np.float64)
    return np.moveaxis((codes * scale).reshape(v.shape), -1, axis)


WIDE = False


def mx_kscale(k):
    if not WIDE:
        return np.ones(k)
    levels = np.array([30, -30])
    if k % 512:
        return np.exp2(np.random.permutation(np.resize(levels, k // 32))).repeat(32)
    a = np.empty((k // 512, 16))
    for p in range(k // 512):
        a[p, :8] = np.random.permutation(np.resize(levels, 8))
        for g in range(8):
            far = levels[np.abs(levels - a[p, g]) >= 10]
            a[p, g + 8] = far[np.random.randint(len(far))]
    return np.exp2(a.ravel()).repeat(32)


def f64(x):
    return np.asarray(x).astype(np.float64)


def striped(idx):
    return np.tile(np.asarray(idx).reshape(-1, 16).T, (8, 1)).astype(np.uint16)


def unstriped(offs):
    return offs[:16].T.reshape(-1).astype(np.int64)


E2M1 = np.array([0.0, 0.5, 1.0, 1.5, 2.0, 3.0, 4.0, 6.0, -0.0, -0.5, -1.0, -1.5, -2.0, -3.0, -4.0, -6.0])


def pack_weight(w, fmt):
    k, n = w.shape
    w = f64(np.asarray(w, np.float32).astype(ml_dtypes.bfloat16)).reshape(k // 32, 32, n)
    amax = np.abs(w).max(1)
    if fmt in ("e4m3", "e5m2"):
        byte = np.frexp(amax)[1] - 1 + 127 - (7 if fmt == "e4m3" else 14)
    else:
        mant, ex = np.frexp(amax / 6.0)
        byte = np.where(mant > 0.5, ex, ex - 1) + 127
    byte = np.clip(np.where(amax > 0, byte, 1), 1, 254)
    scaled = (w * np.exp2(127.0 - byte)[:, None, :]).reshape(k, n).astype(np.float32)
    by_word = np.ascontiguousarray(scaled.reshape(k // 512, 128, 4, n).transpose(0, 1, 3, 2))
    if fmt in ("e4m3", "e5m2"):
        words = by_word.astype(ml_dtypes.float8_e4m3fn if fmt == "e4m3" else ml_dtypes.float8_e5m2).view(np.uint8)
    else:
        c = by_word.astype(ml_dtypes.float4_e2m1fn).view(np.uint8) & 0xF
        words = (c[..., 0::2] | (c[..., 1::2] << 4)).reshape(k // 512, 128, 2 * n)
    return np.ascontiguousarray(words), np.ascontiguousarray(byte.astype(np.uint8).reshape(k // 512, 16, n))


def unpack_weight(words, scales, fmt):
    g, _, n = scales.shape
    words = np.ascontiguousarray(words).reshape(g, 128, n, -1)
    if fmt in ("e4m3", "e5m2"):
        vals = words.view(ml_dtypes.float8_e4m3fn if fmt == "e4m3" else ml_dtypes.float8_e5m2).astype(np.float64)
    else:
        nib = np.empty((g, 128, n, 4), np.uint8)
        nib[..., 0::2] = words & 0xF
        nib[..., 1::2] = words >> 4
        vals = E2M1[nib]
    vals = vals * np.repeat(np.exp2(scales.astype(np.float64) - 127.0), 8, axis=1)[..., None]
    return vals.transpose(0, 1, 3, 2).reshape(g * 512, n)


K, T, J, I, L = 1024, 1024, 256, 256, 512


def setup_inputs():
    n = np.random.standard_normal
    idx = np.random.permutation(T)[:J]
    fk = mx_kscale(K)
    fl = mx_kscale(L)
    xtp = pack_weight(n((K, T)) * 0.04 * fk[:, None], "e5m2")
    cxp = pack_weight(n((L, J)) / fl[:, None], "e2m1")
    wcp = pack_weight(n((L, I)) * 1 / np.sqrt(L) * fl[:, None], "e4m3")
    return {
        "xt_words": xtp[0],
        "xt_scales": xtp[1],
        "ky": (n((K, I)) / fk[:, None]).astype(np.float32),
        "bi": (np.random.uniform(-0.7, 0.7, (1, I))).astype(np.float32),
        "cx_words": cxp[0],
        "cx_scales": cxp[1],
        "wc_words": wcp[0],
        "wc_scales": wcp[1],
        "offs": striped(idx),
    }


def reference(xt_words, xt_scales, ky, bi, cx_words, cx_scales, wc_words, wc_scales, offs):
    idx = unstriped(offs)
    xtu = unpack_weight(xt_words, xt_scales, "e5m2")
    cxu = unpack_weight(cx_words, cx_scales, "e2m1")
    wcu = unpack_weight(wc_words, wc_scales, "e4m3")
    xtidxg = xtu[:, idx]
    kyq = mxq(f64(ky), 0, "e4m3")
    a0 = xtidxg.T @ kyq
    a = a0 + f64(bi)
    q = cxu.T @ wcu
    y = np.maximum(a, q) - 0.5 * np.minimum(a, q)
    return y

@@ -1,0 +1,155 @@
+from contextlib import ExitStack
+
+import concourse.mybir as mybir
+from concourse.masks import make_identity
+
+K, T, J, I, L = 1024, 1024, 256, 256, 512
+FLOPS = 2 * J * I * (K + L)
+
+F32 = mybir.dt.float32
+BF16 = mybir.dt.bfloat16
+I32 = mybir.dt.int32
+U32 = mybir.dt.uint32
+U16 = mybir.dt.uint16
+U8 = mybir.dt.uint8
+E4M3X4 = mybir.dt.float8_e4m3fn_x4
+E5M2X4 = mybir.dt.float8_e5m2_x4
+E2M1X4 = mybir.dt.float4_e2m1fn_x4
+ALU = mybir.AluOpType
+
+P = 128
+PACK = 4
+PASSES = 2
+ROW_TILES = 2
+
+
+def tile_list_scores_picked_given_tworank_kernel(
+    tc, xt_words, xt_scales, ky, bi, cx_words, cx_scales, wc_words, wc_scales, offs, out
+):
+    nc = tc.nc
+    with ExitStack() as ctx:
+        sb = ctx.enter_context(tc.tile_pool(name="sb", bufs=1))
+        ps = ctx.enter_context(tc.psum_pool(name="ps", bufs=1))
+
+        offsets = sb.tile([P, J // 16], U16, name="offsets")
+        bias_cols = sb.tile([P, 2], F32, name="bias_cols")
+        ky_raw = [sb.tile([P, PACK, I], F32, name=f"ky_raw{z}", align_bytes=64) for z in range(PASSES)]
+        xt_table = [sb.tile([P, T], I32, name=f"xt_table{z}", align_bytes=64) for z in range(PASSES)]
+        xt_plane = sb.tile([P, PASSES, T], U8, name="xt_plane", align_bytes=64)
+        ctx_planes = sb.tile([P, J + I], U8, name="ctx_planes", align_bytes=64)
+        cx_codes = sb.tile([P, 2 * J], U8, name="cx_codes", align_bytes=64)
+        wc_codes = sb.tile([P, I], I32, name="wc_codes", align_bytes=64)
+        identity = sb.tile([P, P], F32, name="identity", align_bytes=64)
+
+        nc.vector.memset(xt_plane[:].rearrange("p z c -> p (z c)").bitcast(I32), 0)
+
+        nc.gpsimd.dma_start(out=ctx_planes[0:32, 0:J].bitcast(I32), in_=cx_scales[0, 0:4, :].bitcast(I32).unsqueeze(0).to_broadcast([8, 4, 64]))
+        nc.gpsimd.dma_start(out=ctx_planes[32:64, 0:J].bitcast(I32), in_=cx_scales[0, 4:8, :].bitcast(I32).unsqueeze(0).to_broadcast([8, 4, 64]))
+        nc.gpsimd.dma_start(out=ctx_planes[64:96, 0:J].bitcast(I32), in_=cx_scales[0, 8:12, :].bitcast(I32).unsqueeze(0).to_broadcast([8, 4, 64]))
+        nc.gpsimd.dma_start(out=ctx_planes[96:128, 0:J].bitcast(I32), in_=cx_scales[0, 12:16, :].bitcast(I32).unsqueeze(0).to_broadcast([8, 4, 64]))
+        nc.sync.dma_start(offsets[:], offs)
+        nc.scalar.dma_start(out=ctx_planes[0:32, J:J + I].bitcast(I32), in_=wc_scales[0, 0:4, :].bitcast(I32).unsqueeze(0).to_broadcast([8, 4, 64]))
+        nc.sync.dma_start(out=cx_codes[:].bitcast(I32), in_=cx_words[0].bitcast(I32))
+        nc.scalar.dma_start(out=ky_raw[0][:], in_=ky[0:512, :].rearrange("(p t) i -> p t i", t=PACK))
+        nc.sync.dma_start(out=wc_codes[:], in_=wc_words[0].rearrange("p c t -> p (c t)").bitcast(I32))
+        nc.sync.dma_start(out=bias_cols[:], in_=bi.rearrange("o (p c) -> (o p) c", c=2))
+        nc.sync.dma_start(out=ctx_planes[32:64, J:J + I].bitcast(I32), in_=wc_scales[0, 4:8, :].bitcast(I32).unsqueeze(0).to_broadcast([8, 4, 64]))
+        nc.sync.dma_start(out=ctx_planes[64:96, J:J + I].bitcast(I32), in_=wc_scales[0, 8:12, :].bitcast(I32).unsqueeze(0).to_broadcast([8, 4, 64]))
+        nc.sync.dma_start(out=ctx_planes[96:128, J:J + I].bitcast(I32), in_=wc_scales[0, 12:16, :].bitcast(I32).unsqueeze(0).to_broadcast([8, 4, 64]))
+        nc.sync.dma_start(out=ky_raw[1][:], in_=ky[512:1024, :].rearrange("(p t) i -> p t i", t=PACK))
+        nc.sync.dma_start(out=xt_table[0][:], in_=xt_words[0].rearrange("p c t -> p (c t)").bitcast(I32))
+        nc.sync.dma_start(out=xt_table[1][:], in_=xt_words[1].rearrange("p c t -> p (c t)").bitcast(I32))
+        nc.scalar.dma_start(out=xt_plane[0:4, :, :].bitcast(I32), in_=xt_scales[:, 0:4, :].rearrange("z r c -> r z c").bitcast(I32))
+        nc.scalar.dma_start(out=xt_plane[32:36, :, :].bitcast(I32), in_=xt_scales[:, 4:8, :].rearrange("z r c -> r z c").bitcast(I32))
+        nc.scalar.dma_start(out=xt_plane[64:68, :, :].bitcast(I32), in_=xt_scales[:, 8:12, :].rearrange("z r c -> r z c").bitcast(I32))
+        nc.scalar.dma_start(out=xt_plane[96:100, :, :].bitcast(I32), in_=xt_scales[:, 12:16, :].rearrange("z r c -> r z c").bitcast(I32))
+
+        make_identity(nc, identity[:])
+        bias_ps = ps.tile([P, 2, P], F32, name="bias_ps")
+        for c in range(2):
+            nc.tensor.transpose(bias_ps[:, c, :], bias_cols[:, c : c + 1].to_broadcast([P, P]), identity[:])
+        bias_sb = sb.tile([P, P, 2], F32, name="bias_sb", align_bytes=64)
+        nc.scalar.copy(out=bias_sb[:], in_=bias_ps[:].rearrange("p c n -> p n c"))
+
+        xt_bytes = [sb.tile([P, J], U8, name=f"xt_bytes{z}", align_bytes=64) for z in range(PASSES)]
+        for z in range(PASSES):
+            nc.vector.tensor_copy(xt_bytes[z][:], xt_plane[:, z, :].indirect(offsets[:]))
+
+        ky_bf = [sb.tile([P, I, PACK], BF16, name=f"ky_bf{z}", align_bytes=64) for z in range(PASSES)]
+        ky_codes = [sb.tile([P, I], U32, name=f"ky_codes{z}", align_bytes=64) for z in range(PASSES)]
+        ky_plane = [sb.tile([P, I], U8, name=f"ky_plane{z}", align_bytes=64) for z in range(PASSES)]
+
+        def quantize_keys(z):
+            (nc.vector.tensor_copy if z == 0 else nc.scalar.copy)(
+                out=ky_bf[z][:].rearrange("p (c n) t -> p c t n", n=4),
+                in_=ky_raw[z][:].rearrange("p t (c n) -> p c t n", n=4),
+            )
+            nc.vector.quantize_mx(
+                out=ky_codes[z][:].bitcast(E4M3X4),
+                scales=ky_plane[z][:],
+                in_=ky_bf[z][:].rearrange("p i t -> p (i t)"),
+            )
+
+        quantize_keys(0)
+
+        q_ps = ps.tile([P, ROW_TILES, I], F32, name="q_ps")
+        for h in range(ROW_TILES):
+            nc.tensor.matmul_mx(
+                out=q_ps[:, h, :],
+                lhsT=cx_codes[:, 2 * P * h : 2 * P * (h + 1)].bitcast(E2M1X4),
+                lhsT_scale=ctx_planes[:, P * h : P * (h + 1)],
+                rhs=wc_codes[:].bitcast(E4M3X4),
+                rhs_scale=ctx_planes[:, J : J + I],
+                start=True,
+                stop=True,
+            )
+        u_sb = sb.tile([P, ROW_TILES, I], F32, name="u_sb", align_bytes=64)
+        bias_row = bias_sb[:].rearrange("p n c -> p (n c)")
+        nc.vector.scalar_tensor_tensor(
+            out=u_sb[:],
+            in0=q_ps[:],
+            scalar=-0.5,
+            in1=bias_row.unsqueeze(1).to_broadcast([P, ROW_TILES, I]),
+            op0=ALU.mult,
+            op1=ALU.add,
+        )
+
+        quantize_keys(1)
+
+        a_ps = [ps.tile([P, I], F32, name=f"a_ps{h}") for h in range(ROW_TILES)]
+
+        def score_pass(z, h, picked):
+            nc.tensor.matmul_mx(
+                out=a_ps[h][:],
+                lhsT=picked.bitcast(E5M2X4),
+                lhsT_scale=xt_bytes[z][:, P * h : P * (h + 1)],
+                rhs=ky_codes[z][:].bitcast(E4M3X4),
+                rhs_scale=ky_plane[z][:],
+                start=(z == 0),
+                stop=(z == PASSES - 1),
+            )
+
+        picked0 = sb.tile([P, J], U32, name="picked0", align_bytes=64)
+        nc.vector.tensor_copy(picked0[:], xt_table[0][:].bitcast(U32).indirect(offsets[:]))
+        for h in range(ROW_TILES):
+            score_pass(0, h, picked0[:, P * h : P * (h + 1)])
+        for h in range(ROW_TILES):
+            picked1 = sb.tile([P, P], U32, name=f"picked1_{h}", align_bytes=64)
+            nc.vector.tensor_copy(picked1[:], xt_table[1][:].bitcast(U32).indirect(offsets[:, 8 * h : 8 * (h + 1)]))
+            score_pass(1, h, picked1[:])
+
+        s_sb = [sb.tile([P, I], F32, name=f"s_sb{h}", align_bytes=64) for h in range(ROW_TILES)]
+        t_sb = [sb.tile([P, I], F32, name=f"t_sb{h}", align_bytes=64) for h in range(ROW_TILES)]
+        y_sb = [sb.tile([P, I], F32, name=f"y_sb{h}", align_bytes=64) for h in range(ROW_TILES)]
+        for h in range(ROW_TILES):
+            nc.vector.tensor_tensor(out=s_sb[h][:], in0=a_ps[h][:], in1=u_sb[:, h, :], op=ALU.add)
+        for h in range(ROW_TILES):
+            nc.vector.scalar_tensor_tensor(
+                out=t_sb[h][:], in0=q_ps[:, h, :], scalar=-1.5, in1=s_sb[h][:], op0=ALU.mult, op1=ALU.add
+            )
+        for h in range(ROW_TILES):
+            nc.vector.scalar_tensor_tensor(
+                out=y_sb[h][:], in0=t_sb[h][:], scalar=-0.5, in1=s_sb[h][:], op0=ALU.mult, op1=ALU.max
+            )
+        nc.scalar.dma_start(out=out[0:P, :], in_=y_sb[0][:])
+        nc.sync.dma_start(out=out[P : 2 * P, :], in_=y_sb[1][:])

@@ -34,7 +34,7 @@ def tile_list_scores_picked_given_tworank_kernel(
         offsets = sb.tile([P, J // 16], U16, name="offsets")
         bias_cols = sb.tile([P, 2], F32, name="bias_cols")
         ky_raw = [sb.tile([P, PACK, I], F32, name=f"ky_raw{z}", align_bytes=64) for z in range(PASSES)]
-        xt_table = [sb.tile([P, T], I32, name=f"xt_table{z}", align_bytes=64) for z in range(PASSES)]
+        xt_table = [sb.tile([P, T], I32, name=f"xt_table{z}", tag=f"table{z}", align_bytes=64) for z in range(PASSES)]
         xt_plane = sb.tile([P, PASSES, T], U8, name="xt_plane", align_bytes=64)
         ctx_planes = sb.tile([P, J + I], U8, name="ctx_planes", align_bytes=64)
         cx_codes = sb.tile([P, 2 * J], U8, name="cx_codes", align_bytes=64)
@@ -42,29 +42,29 @@ def tile_list_scores_picked_given_tworank_kernel(
         identity = sb.tile([P, P], F32, name="identity", align_bytes=64)
 
         nc.vector.memset(xt_plane[:].rearrange("p z c -> p (z c)").bitcast(I32), 0)
+        make_identity(nc, identity[:])
 
-        nc.gpsimd.dma_start(out=ctx_planes[0:32, 0:J].bitcast(I32), in_=cx_scales[0, 0:4, :].bitcast(I32).unsqueeze(0).to_broadcast([8, 4, 64]))
-        nc.gpsimd.dma_start(out=ctx_planes[32:64, 0:J].bitcast(I32), in_=cx_scales[0, 4:8, :].bitcast(I32).unsqueeze(0).to_broadcast([8, 4, 64]))
-        nc.gpsimd.dma_start(out=ctx_planes[64:96, 0:J].bitcast(I32), in_=cx_scales[0, 8:12, :].bitcast(I32).unsqueeze(0).to_broadcast([8, 4, 64]))
-        nc.gpsimd.dma_start(out=ctx_planes[96:128, 0:J].bitcast(I32), in_=cx_scales[0, 12:16, :].bitcast(I32).unsqueeze(0).to_broadcast([8, 4, 64]))
-        nc.sync.dma_start(offsets[:], offs)
-        nc.scalar.dma_start(out=ctx_planes[0:32, J:J + I].bitcast(I32), in_=wc_scales[0, 0:4, :].bitcast(I32).unsqueeze(0).to_broadcast([8, 4, 64]))
         nc.sync.dma_start(out=cx_codes[:].bitcast(I32), in_=cx_words[0].bitcast(I32))
-        nc.scalar.dma_start(out=ky_raw[0][:], in_=ky[0:512, :].rearrange("(p t) i -> p t i", t=PACK))
+        nc.scalar.dma_start(out=bias_cols[:], in_=bi.rearrange("o (p c) -> (o p) c", c=2))
         nc.sync.dma_start(out=wc_codes[:], in_=wc_words[0].rearrange("p c t -> p (c t)").bitcast(I32))
-        nc.sync.dma_start(out=bias_cols[:], in_=bi.rearrange("o (p c) -> (o p) c", c=2))
+        nc.scalar.dma_start(out=ctx_planes[0:32, 0:J].bitcast(I32), in_=cx_scales[0, 0:4, :].bitcast(I32).unsqueeze(0).to_broadcast([8, 4, 64]))
+        nc.scalar.dma_start(out=ctx_planes[32:64, 0:J].bitcast(I32), in_=cx_scales[0, 4:8, :].bitcast(I32).unsqueeze(0).to_broadcast([8, 4, 64]))
+        nc.sync.dma_start(offsets[:], offs)
+        nc.scalar.dma_start(out=ctx_planes[64:96, 0:J].bitcast(I32), in_=cx_scales[0, 8:12, :].bitcast(I32).unsqueeze(0).to_broadcast([8, 4, 64]))
+        nc.sync.dma_start(out=ky_raw[0][:], in_=ky[0:512, :].rearrange("(p t) i -> p t i", t=PACK))
+        nc.sync.dma_start(out=xt_plane[0:4, :, :].bitcast(I32), in_=xt_scales[:, 0:4, :].rearrange("z r c -> r z c").bitcast(I32))
+        nc.sync.dma_start(out=xt_plane[32:36, :, :].bitcast(I32), in_=xt_scales[:, 4:8, :].rearrange("z r c -> r z c").bitcast(I32))
+        nc.sync.dma_start(out=xt_plane[64:68, :, :].bitcast(I32), in_=xt_scales[:, 8:12, :].rearrange("z r c -> r z c").bitcast(I32))
+        nc.sync.dma_start(out=xt_plane[96:100, :, :].bitcast(I32), in_=xt_scales[:, 12:16, :].rearrange("z r c -> r z c").bitcast(I32))
+        nc.sync.dma_start(out=ky_raw[1][:], in_=ky[512:1024, :].rearrange("(p t) i -> p t i", t=PACK))
+        nc.sync.dma_start(out=ctx_planes[96:128, 0:J].bitcast(I32), in_=cx_scales[0, 12:16, :].bitcast(I32).unsqueeze(0).to_broadcast([8, 4, 64]))
+        nc.sync.dma_start(out=ctx_planes[0:32, J:J + I].bitcast(I32), in_=wc_scales[0, 0:4, :].bitcast(I32).unsqueeze(0).to_broadcast([8, 4, 64]))
         nc.sync.dma_start(out=ctx_planes[32:64, J:J + I].bitcast(I32), in_=wc_scales[0, 4:8, :].bitcast(I32).unsqueeze(0).to_broadcast([8, 4, 64]))
         nc.sync.dma_start(out=ctx_planes[64:96, J:J + I].bitcast(I32), in_=wc_scales[0, 8:12, :].bitcast(I32).unsqueeze(0).to_broadcast([8, 4, 64]))
         nc.sync.dma_start(out=ctx_planes[96:128, J:J + I].bitcast(I32), in_=wc_scales[0, 12:16, :].bitcast(I32).unsqueeze(0).to_broadcast([8, 4, 64]))
-        nc.sync.dma_start(out=ky_raw[1][:], in_=ky[512:1024, :].rearrange("(p t) i -> p t i", t=PACK))
         nc.sync.dma_start(out=xt_table[0][:], in_=xt_words[0].rearrange("p c t -> p (c t)").bitcast(I32))
         nc.sync.dma_start(out=xt_table[1][:], in_=xt_words[1].rearrange("p c t -> p (c t)").bitcast(I32))
-        nc.scalar.dma_start(out=xt_plane[0:4, :, :].bitcast(I32), in_=xt_scales[:, 0:4, :].rearrange("z r c -> r z c").bitcast(I32))
-        nc.scalar.dma_start(out=xt_plane[32:36, :, :].bitcast(I32), in_=xt_scales[:, 4:8, :].rearrange("z r c -> r z c").bitcast(I32))
-        nc.scalar.dma_start(out=xt_plane[64:68, :, :].bitcast(I32), in_=xt_scales[:, 8:12, :].rearrange("z r c -> r z c").bitcast(I32))
-        nc.scalar.dma_start(out=xt_plane[96:100, :, :].bitcast(I32), in_=xt_scales[:, 12:16, :].rearrange("z r c -> r z c").bitcast(I32))
 
-        make_identity(nc, identity[:])
         bias_ps = ps.tile([P, 2, P], F32, name="bias_ps")
         for c in range(2):
             nc.tensor.transpose(bias_ps[:, c, :], bias_cols[:, c : c + 1].to_broadcast([P, P]), identity[:])
@@ -80,7 +80,7 @@ def tile_list_scores_picked_given_tworank_kernel(
         ky_plane = [sb.tile([P, I], U8, name=f"ky_plane{z}", align_bytes=64) for z in range(PASSES)]
 
         def quantize_keys(z):
-            (nc.vector.tensor_copy if z == 0 else nc.scalar.copy)(
+            nc.scalar.copy(
                 out=ky_bf[z][:].rearrange("p (c n) t -> p c t n", n=4),
                 in_=ky_raw[z][:].rearrange("p t (c n) -> p c t n", n=4),
             )
@@ -103,16 +103,6 @@ def tile_list_scores_picked_given_tworank_kernel(
                 start=True,
                 stop=True,
             )
-        u_sb = sb.tile([P, ROW_TILES, I], F32, name="u_sb", align_bytes=64)
-        bias_row = bias_sb[:].rearrange("p n c -> p (n c)")
-        nc.vector.scalar_tensor_tensor(
-            out=u_sb[:],
-            in0=q_ps[:],
-            scalar=-0.5,
-            in1=bias_row.unsqueeze(1).to_broadcast([P, ROW_TILES, I]),
-            op0=ALU.mult,
-            op1=ALU.add,
-        )
 
         quantize_keys(1)
 
@@ -133,6 +123,12 @@ def tile_list_scores_picked_given_tworank_kernel(
         nc.vector.tensor_copy(picked0[:], xt_table[0][:].bitcast(U32).indirect(offsets[:]))
         for h in range(ROW_TILES):
             score_pass(0, h, picked0[:, P * h : P * (h + 1)])
+        u_sb = sb.tile([P, ROW_TILES, I], F32, name="u_sb", tag="table0", align_bytes=64)
+        bias_row = bias_sb[:].rearrange("p n c -> p (n c)")
+        for h in range(ROW_TILES):
+            nc.vector.scalar_tensor_tensor(
+                out=u_sb[:, h, :], in0=q_ps[:, h, :], scalar=-0.5, in1=bias_row, op0=ALU.mult, op1=ALU.add
+            )
         for h in range(ROW_TILES):
             picked1 = sb.tile([P, P], U32, name=f"picked1_{h}", align_bytes=64)
             nc.vector.tensor_copy(picked1[:], xt_table[1][:].bitcast(U32).indirect(offsets[:, 8 * h : 8 * (h + 1)]))

@@ -34,46 +34,49 @@ def tile_list_scores_picked_given_tworank_kernel(
         offsets = sb.tile([P, J // 16], U16, name="offsets")
         bias_cols = sb.tile([P, 2], F32, name="bias_cols")
         ky_raw = [sb.tile([P, PACK, I], F32, name=f"ky_raw{z}", align_bytes=64) for z in range(PASSES)]
-        xt_table = [sb.tile([P, T], I32, name=f"xt_table{z}", tag=f"table{z}", align_bytes=64) for z in range(PASSES)]
-        xt_plane = sb.tile([P, PASSES, T], U8, name="xt_plane", align_bytes=64)
+        xt_table = [sb.tile([P, T], I32, name="xt_table0", align_bytes=64)]
+        xt_rows = sb.tile([P, T], U8, name="xt_rows", tag="table1", align_bytes=64)
+        xt_planes = sb.tile([P, PASSES * J], U8, name="xt_planes", align_bytes=64)
         ctx_planes = sb.tile([P, J + I], U8, name="ctx_planes", align_bytes=64)
         cx_codes = sb.tile([P, 2 * J], U8, name="cx_codes", align_bytes=64)
         wc_codes = sb.tile([P, I], I32, name="wc_codes", align_bytes=64)
         identity = sb.tile([P, P], F32, name="identity", align_bytes=64)
 
-        nc.vector.memset(xt_plane[:].rearrange("p z c -> p (z c)").bitcast(I32), 0)
+        nc.vector.memset(xt_rows[:].bitcast(I32), 0)
+        nc.vector.memset(xt_planes[:].bitcast(I32), 0)
         make_identity(nc, identity[:])
 
         nc.sync.dma_start(out=cx_codes[:].bitcast(I32), in_=cx_words[0].bitcast(I32))
         nc.scalar.dma_start(out=bias_cols[:], in_=bi.rearrange("o (p c) -> (o p) c", c=2))
         nc.sync.dma_start(out=wc_codes[:], in_=wc_words[0].rearrange("p c t -> p (c t)").bitcast(I32))
         nc.scalar.dma_start(out=ctx_planes[0:32, 0:J].bitcast(I32), in_=cx_scales[0, 0:4, :].bitcast(I32).unsqueeze(0).to_broadcast([8, 4, 64]))
-        nc.scalar.dma_start(out=ctx_planes[32:64, 0:J].bitcast(I32), in_=cx_scales[0, 4:8, :].bitcast(I32).unsqueeze(0).to_broadcast([8, 4, 64]))
         nc.sync.dma_start(offsets[:], offs)
-        nc.scalar.dma_start(out=ctx_planes[64:96, 0:J].bitcast(I32), in_=cx_scales[0, 8:12, :].bitcast(I32).unsqueeze(0).to_broadcast([8, 4, 64]))
+        nc.scalar.dma_start(out=xt_rows[0:32, :].bitcast(I32), in_=xt_scales.rearrange("z b c -> b z c").bitcast(I32))
+        nc.sync.dma_start(out=ctx_planes[32:64, 0:J].bitcast(I32), in_=cx_scales[0, 4:8, :].bitcast(I32).unsqueeze(0).to_broadcast([8, 4, 64]))
         nc.sync.dma_start(out=ky_raw[0][:], in_=ky[0:512, :].rearrange("(p t) i -> p t i", t=PACK))
-        nc.sync.dma_start(out=xt_plane[0:4, :, :].bitcast(I32), in_=xt_scales[:, 0:4, :].rearrange("z r c -> r z c").bitcast(I32))
-        nc.sync.dma_start(out=xt_plane[32:36, :, :].bitcast(I32), in_=xt_scales[:, 4:8, :].rearrange("z r c -> r z c").bitcast(I32))
-        nc.sync.dma_start(out=xt_plane[64:68, :, :].bitcast(I32), in_=xt_scales[:, 8:12, :].rearrange("z r c -> r z c").bitcast(I32))
-        nc.sync.dma_start(out=xt_plane[96:100, :, :].bitcast(I32), in_=xt_scales[:, 12:16, :].rearrange("z r c -> r z c").bitcast(I32))
-        nc.sync.dma_start(out=ky_raw[1][:], in_=ky[512:1024, :].rearrange("(p t) i -> p t i", t=PACK))
+        nc.sync.dma_start(out=ctx_planes[64:96, 0:J].bitcast(I32), in_=cx_scales[0, 8:12, :].bitcast(I32).unsqueeze(0).to_broadcast([8, 4, 64]))
         nc.sync.dma_start(out=ctx_planes[96:128, 0:J].bitcast(I32), in_=cx_scales[0, 12:16, :].bitcast(I32).unsqueeze(0).to_broadcast([8, 4, 64]))
         nc.sync.dma_start(out=ctx_planes[0:32, J:J + I].bitcast(I32), in_=wc_scales[0, 0:4, :].bitcast(I32).unsqueeze(0).to_broadcast([8, 4, 64]))
         nc.sync.dma_start(out=ctx_planes[32:64, J:J + I].bitcast(I32), in_=wc_scales[0, 4:8, :].bitcast(I32).unsqueeze(0).to_broadcast([8, 4, 64]))
         nc.sync.dma_start(out=ctx_planes[64:96, J:J + I].bitcast(I32), in_=wc_scales[0, 8:12, :].bitcast(I32).unsqueeze(0).to_broadcast([8, 4, 64]))
         nc.sync.dma_start(out=ctx_planes[96:128, J:J + I].bitcast(I32), in_=wc_scales[0, 12:16, :].bitcast(I32).unsqueeze(0).to_broadcast([8, 4, 64]))
+        nc.sync.dma_start(out=ky_raw[1][:], in_=ky[512:1024, :].rearrange("(p t) i -> p t i", t=PACK))
         nc.sync.dma_start(out=xt_table[0][:], in_=xt_words[0].rearrange("p c t -> p (c t)").bitcast(I32))
-        nc.sync.dma_start(out=xt_table[1][:], in_=xt_words[1].rearrange("p c t -> p (c t)").bitcast(I32))
 
-        bias_ps = ps.tile([P, 2, P], F32, name="bias_ps")
+        bias_ps = ps.tile([P, 2, P], F32, name="bias_ps", tag="context")
         for c in range(2):
             nc.tensor.transpose(bias_ps[:, c, :], bias_cols[:, c : c + 1].to_broadcast([P, P]), identity[:])
         bias_sb = sb.tile([P, P, 2], F32, name="bias_sb", align_bytes=64)
         nc.scalar.copy(out=bias_sb[:], in_=bias_ps[:].rearrange("p c n -> p n c"))
 
-        xt_bytes = [sb.tile([P, J], U8, name=f"xt_bytes{z}", align_bytes=64) for z in range(PASSES)]
-        for z in range(PASSES):
-            nc.vector.tensor_copy(xt_bytes[z][:], xt_plane[:, z, :].indirect(offsets[:]))
+        xt_bytes = sb.tile([P, J], U8, name="xt_bytes", align_bytes=64)
+        nc.vector.tensor_copy(xt_bytes[:], xt_rows[:].indirect(offsets[:]))
+        for qd in range(4):
+            nc.sync.dma_start(
+                out=xt_planes[32 * qd : 32 * qd + 4, :].bitcast(I32), in_=xt_bytes[8 * qd : 8 * qd + 8, :].bitcast(I32)
+            )
+        xt_table.append(sb.tile([P, T], I32, name="xt_table1", tag="table1", align_bytes=64))
+        nc.sync.dma_start(out=xt_table[1][:], in_=xt_words[1].rearrange("p c t -> p (c t)").bitcast(I32))
 
         ky_bf = [sb.tile([P, I, PACK], BF16, name=f"ky_bf{z}", align_bytes=64) for z in range(PASSES)]
         ky_codes = [sb.tile([P, I], U32, name=f"ky_codes{z}", align_bytes=64) for z in range(PASSES)]
@@ -92,7 +95,7 @@ def tile_list_scores_picked_given_tworank_kernel(
 
         quantize_keys(0)
 
-        q_ps = ps.tile([P, ROW_TILES, I], F32, name="q_ps")
+        q_ps = ps.tile([P, ROW_TILES, I], F32, name="q_ps", tag="context")
         for h in range(ROW_TILES):
             nc.tensor.matmul_mx(
                 out=q_ps[:, h, :],
@@ -103,6 +106,12 @@ def tile_list_scores_picked_given_tworank_kernel(
                 start=True,
                 stop=True,
             )
+        u_sb = sb.tile([P, ROW_TILES, I], F32, name="u_sb", align_bytes=64)
+        bias_row = bias_sb[:].rearrange("p n c -> p (n c)")
+        for h in range(ROW_TILES):
+            nc.vector.scalar_tensor_tensor(
+                out=u_sb[:, h, :], in0=q_ps[:, h, :], scalar=-0.5, in1=bias_row, op0=ALU.mult, op1=ALU.add
+            )
 
         quantize_keys(1)
 
@@ -112,7 +121,7 @@ def tile_list_scores_picked_given_tworank_kernel(
             nc.tensor.matmul_mx(
                 out=a_ps[h][:],
                 lhsT=picked.bitcast(E5M2X4),
-                lhsT_scale=xt_bytes[z][:, P * h : P * (h + 1)],
+                lhsT_scale=xt_planes[:, J * z + P * h : J * z + P * (h + 1)],
                 rhs=ky_codes[z][:].bitcast(E4M3X4),
                 rhs_scale=ky_plane[z][:],
                 start=(z == 0),
@@ -123,12 +132,6 @@ def tile_list_scores_picked_given_tworank_kernel(
         nc.vector.tensor_copy(picked0[:], xt_table[0][:].bitcast(U32).indirect(offsets[:]))
         for h in range(ROW_TILES):
             score_pass(0, h, picked0[:, P * h : P * (h + 1)])
-        u_sb = sb.tile([P, ROW_TILES, I], F32, name="u_sb", tag="table0", align_bytes=64)
-        bias_row = bias_sb[:].rearrange("p n c -> p (n c)")
-        for h in range(ROW_TILES):
-            nc.vector.scalar_tensor_tensor(
-                out=u_sb[:, h, :], in0=q_ps[:, h, :], scalar=-0.5, in1=bias_row, op0=ALU.mult, op1=ALU.add
-            )
         for h in range(ROW_TILES):
             picked1 = sb.tile([P, P], U32, name=f"picked1_{h}", align_bytes=64)
             nc.vector.tensor_copy(picked1[:], xt_table[1][:].bitcast(U32).indirect(offsets[:, 8 * h : 8 * (h + 1)]))

from contextlib import ExitStack

import concourse.mybir as mybir
from concourse.masks import make_identity

K, T, J, I, L = 1024, 1024, 256, 256, 512
FLOPS = 2 * J * I * (K + L)

F32 = mybir.dt.float32
BF16 = mybir.dt.bfloat16
I32 = mybir.dt.int32
U32 = mybir.dt.uint32
U16 = mybir.dt.uint16
U8 = mybir.dt.uint8
E4M3X4 = mybir.dt.float8_e4m3fn_x4
E5M2X4 = mybir.dt.float8_e5m2_x4
E2M1X4 = mybir.dt.float4_e2m1fn_x4
ALU = mybir.AluOpType

P = 128
PACK = 4
PASSES = 2
ROW_TILES = 2


def tile_list_scores_picked_given_tworank_kernel(
    tc, xt_words, xt_scales, ky, bi, cx_words, cx_scales, wc_words, wc_scales, offs, out
):
    nc = tc.nc
    with ExitStack() as ctx:
        sb = ctx.enter_context(tc.tile_pool(name="sb", bufs=1))
        ps = ctx.enter_context(tc.psum_pool(name="ps", bufs=1))

        offsets = sb.tile([P, J // 16], U16, name="offsets")
        bias_cols = sb.tile([P, 2], F32, name="bias_cols")
        ky_raw = [sb.tile([P, PACK, I], F32, name=f"ky_raw{z}", align_bytes=64) for z in range(PASSES)]
        xt_table = [sb.tile([P, T], I32, name="xt_table0", align_bytes=64)]
        xt_rows = sb.tile([P, T], U8, name="xt_rows", tag="table1", align_bytes=64)
        xt_planes = sb.tile([P, PASSES * J], U8, name="xt_planes", align_bytes=64)
        ctx_planes = sb.tile([P, J + I], U8, name="ctx_planes", align_bytes=64)
        cx_codes = sb.tile([P, 2 * J], U8, name="cx_codes", align_bytes=64)
        wc_codes = sb.tile([P, I], I32, name="wc_codes", align_bytes=64)
        identity = sb.tile([P, P], F32, name="identity", align_bytes=64)

        nc.vector.memset(xt_rows[:].bitcast(I32), 0)
        nc.vector.memset(xt_planes[:].bitcast(I32), 0)
        make_identity(nc, identity[:])

        nc.sync.dma_start(out=cx_codes[:].bitcast(I32), in_=cx_words[0].bitcast(I32))
        nc.scalar.dma_start(out=bias_cols[:], in_=bi.rearrange("o (p c) -> (o p) c", c=2))
        nc.sync.dma_start(out=wc_codes[:], in_=wc_words[0].rearrange("p c t -> p (c t)").bitcast(I32))
        nc.scalar.dma_start(out=ctx_planes[0:32, 0:J].bitcast(I32), in_=cx_scales[0, 0:4, :].bitcast(I32).unsqueeze(0).to_broadcast([8, 4, 64]))
        nc.sync.dma_start(offsets[:], offs)
        nc.scalar.dma_start(out=xt_rows[0:32, :].bitcast(I32), in_=xt_scales.rearrange("z b c -> b z c").bitcast(I32))
        nc.sync.dma_start(out=ctx_planes[32:64, 0:J].bitcast(I32), in_=cx_scales[0, 4:8, :].bitcast(I32).unsqueeze(0).to_broadcast([8, 4, 64]))
        nc.sync.dma_start(out=ky_raw[0][:], in_=ky[0:512, :].rearrange("(p t) i -> p t i", t=PACK))
        nc.sync.dma_start(out=ctx_planes[64:96, 0:J].bitcast(I32), in_=cx_scales[0, 8:12, :].bitcast(I32).unsqueeze(0).to_broadcast([8, 4, 64]))
        nc.sync.dma_start(out=ctx_planes[96:128, 0:J].bitcast(I32), in_=cx_scales[0, 12:16, :].bitcast(I32).unsqueeze(0).to_broadcast([8, 4, 64]))
        nc.sync.dma_start(out=ctx_planes[0:32, J:J + I].bitcast(I32), in_=wc_scales[0, 0:4, :].bitcast(I32).unsqueeze(0).to_broadcast([8, 4, 64]))
        nc.sync.dma_start(out=ctx_planes[32:64, J:J + I].bitcast(I32), in_=wc_scales[0, 4:8, :].bitcast(I32).unsqueeze(0).to_broadcast([8, 4, 64]))
        nc.sync.dma_start(out=ctx_planes[64:96, J:J + I].bitcast(I32), in_=wc_scales[0, 8:12, :].bitcast(I32).unsqueeze(0).to_broadcast([8, 4, 64]))
        nc.sync.dma_start(out=ctx_planes[96:128, J:J + I].bitcast(I32), in_=wc_scales[0, 12:16, :].bitcast(I32).unsqueeze(0).to_broadcast([8, 4, 64]))
        nc.sync.dma_start(out=ky_raw[1][:], in_=ky[512:1024, :].rearrange("(p t) i -> p t i", t=PACK))
        nc.sync.dma_start(out=xt_table[0][:], in_=xt_words[0].rearrange("p c t -> p (c t)").bitcast(I32))

        bias_ps = ps.tile([P, 2, P], F32, name="bias_ps", tag="context")
        for c in range(2):
            nc.tensor.transpose(bias_ps[:, c, :], bias_cols[:, c : c + 1].to_broadcast([P, P]), identity[:])
        bias_sb = sb.tile([P, P, 2], F32, name="bias_sb", align_bytes=64)
        nc.scalar.copy(out=bias_sb[:], in_=bias_ps[:].rearrange("p c n -> p n c"))

        xt_bytes = sb.tile([P, J], U8, name="xt_bytes", align_bytes=64)
        nc.vector.tensor_copy(xt_bytes[:], xt_rows[:].indirect(offsets[:]))
        for qd in range(4):
            nc.sync.dma_start(
                out=xt_planes[32 * qd : 32 * qd + 4, :].bitcast(I32), in_=xt_bytes[8 * qd : 8 * qd + 8, :].bitcast(I32)
            )
        xt_table.append(sb.tile([P, T], I32, name="xt_table1", tag="table1", align_bytes=64))
        nc.sync.dma_start(out=xt_table[1][:], in_=xt_words[1].rearrange("p c t -> p (c t)").bitcast(I32))

        ky_bf = [sb.tile([P, I, PACK], BF16, name=f"ky_bf{z}", align_bytes=64) for z in range(PASSES)]
        ky_codes = [sb.tile([P, I], U32, name=f"ky_codes{z}", align_bytes=64) for z in range(PASSES)]
        ky_plane = [sb.tile([P, I], U8, name=f"ky_plane{z}", align_bytes=64) for z in range(PASSES)]

        def quantize_keys(z):
            nc.scalar.copy(
                out=ky_bf[z][:].rearrange("p (c n) t -> p c t n", n=4),
                in_=ky_raw[z][:].rearrange("p t (c n) -> p c t n", n=4),
            )
            nc.vector.quantize_mx(
                out=ky_codes[z][:].bitcast(E4M3X4),
                scales=ky_plane[z][:],
                in_=ky_bf[z][:].rearrange("p i t -> p (i t)"),
            )

        quantize_keys(0)

        q_ps = ps.tile([P, ROW_TILES, I], F32, name="q_ps", tag="context")
        for h in range(ROW_TILES):
            nc.tensor.matmul_mx(
                out=q_ps[:, h, :],
                lhsT=cx_codes[:, 2 * P * h : 2 * P * (h + 1)].bitcast(E2M1X4),
                lhsT_scale=ctx_planes[:, P * h : P * (h + 1)],
                rhs=wc_codes[:].bitcast(E4M3X4),
                rhs_scale=ctx_planes[:, J : J + I],
                start=True,
                stop=True,
            )
        u_sb = sb.tile([P, ROW_TILES, I], F32, name="u_sb", align_bytes=64)
        bias_row = bias_sb[:].rearrange("p n c -> p (n c)")
        for h in range(ROW_TILES):
            nc.vector.scalar_tensor_tensor(
                out=u_sb[:, h, :], in0=q_ps[:, h, :], scalar=-0.5, in1=bias_row, op0=ALU.mult, op1=ALU.add
            )

        quantize_keys(1)

        a_ps = [ps.tile([P, I], F32, name=f"a_ps{h}") for h in range(ROW_TILES)]

        def score_pass(z, h, picked):
            nc.tensor.matmul_mx(
                out=a_ps[h][:],
                lhsT=picked.bitcast(E5M2X4),
                lhsT_scale=xt_planes[:, J * z + P * h : J * z + P * (h + 1)],
                rhs=ky_codes[z][:].bitcast(E4M3X4),
                rhs_scale=ky_plane[z][:],
                start=(z == 0),
                stop=(z == PASSES - 1),
            )

        picked0 = sb.tile([P, J], U32, name="picked0", align_bytes=64)
        nc.vector.tensor_copy(picked0[:], xt_table[0][:].bitcast(U32).indirect(offsets[:]))
        for h in range(ROW_TILES):
            score_pass(0, h, picked0[:, P * h : P * (h + 1)])
        for h in range(ROW_TILES):
            picked1 = sb.tile([P, P], U32, name=f"picked1_{h}", align_bytes=64)
            nc.vector.tensor_copy(picked1[:], xt_table[1][:].bitcast(U32).indirect(offsets[:, 8 * h : 8 * (h + 1)]))
            score_pass(1, h, picked1[:])

        s_sb = [sb.tile([P, I], F32, name=f"s_sb{h}", align_bytes=64) for h in range(ROW_TILES)]
        t_sb = [sb.tile([P, I], F32, name=f"t_sb{h}", align_bytes=64) for h in range(ROW_TILES)]
        y_sb = [sb.tile([P, I], F32, name=f"y_sb{h}", align_bytes=64) for h in range(ROW_TILES)]
        for h in range(ROW_TILES):
            nc.vector.tensor_tensor(out=s_sb[h][:], in0=a_ps[h][:], in1=u_sb[:, h, :], op=ALU.add)
        for h in range(ROW_TILES):
            nc.vector.scalar_tensor_tensor(
                out=t_sb[h][:], in0=q_ps[:, h, :], scalar=-1.5, in1=s_sb[h][:], op0=ALU.mult, op1=ALU.add
            )
        for h in range(ROW_TILES):
            nc.vector.scalar_tensor_tensor(
                out=y_sb[h][:], in0=t_sb[h][:], scalar=-0.5, in1=s_sb[h][:], op0=ALU.mult, op1=ALU.max
            )
        nc.scalar.dma_start(out=out[0:P, :], in_=y_sb[0][:])
        nc.sync.dma_start(out=out[P : 2 * P, :], in_=y_sb[1][:])
